import numpy as np
import ml_dtypes


def mxq(x, axis, fmt="e4m3"):
    dtype, down = {"e4m3": (ml_dtypes.float8_e4m3fn, 7), "e5m2": (ml_dtypes.float8_e5m2, 14)}[fmt]
    v = np.moveaxis(np.asarray(x, np.float32).astype(ml_dtypes.bfloat16).astype(np.float64), axis, -1)
    blocks = v.reshape(v.shape[:-1] + (-1, 32))
    amax = np.abs(blocks).max(-1, keepdims=True)
    byte = np.maximum(np.where(amax > 0, np.frexp(amax)[1] - 1 + 127, 0) - down, 1)
    scale = np.exp2(byte - 127.0)
    codes = (blocks / scale).astype(np.float32).astype(dtype).astype(np.float64)
    return np.moveaxis((codes * scale).reshape(v.shape), -1, axis)


WIDE = False


def mx_kscale(k):
    if not WIDE:
        return np.ones(k)
    levels = np.array([10, -10, 5, -5, 0])
    if k % 512:
        return np.exp2(np.random.permutation(np.resize(levels, k // 32))).repeat(32)
    a = np.empty((k // 512, 16))
    for p in range(k // 512):
        a[p, :8] = np.random.permutation(np.resize(levels, 8))
        for g in range(8):
            far = levels[np.abs(levels - a[p, g]) >= 10]
            a[p, g + 8] = far[np.random.randint(len(far))]
    return np.exp2(a.ravel()).repeat(32)


def f64(x):
    return np.asarray(x).astype(np.float64)


def striped(idx):
    return np.tile(idx.reshape(-1, 16).T, (8, 1)).astype(np.uint16)


def unstriped(offs):
    return offs[:16].T.reshape(-1).astype(np.int64)


E2M1 = np.array([0.0, 0.5, 1.0, 1.5, 2.0, 3.0, 4.0, 6.0, -0.0, -0.5, -1.0, -1.5, -2.0, -3.0, -4.0, -6.0])


def pack_weight(w, fmt):
    k, n = w.shape
    w = f64(np.asarray(w, np.float32).astype(ml_dtypes.bfloat16)).reshape(k // 32, 32, n)
    amax = np.abs(w).max(1)
    if fmt == "e4m3":
        byte = np.frexp(amax)[1] - 1 + 127 - 7
    else:
        mant, ex = np.frexp(amax / 6.0)
        byte = np.where(mant > 0.5, ex, ex - 1) + 127
    byte = np.clip(np.where(amax > 0, byte, 1), 1, 254)
    scaled = (w * np.exp2(127.0 - byte)[:, None, :]).reshape(k, n).astype(np.float32)
    by_word = np.ascontiguousarray(scaled.reshape(k // 512, 128, 4, n).transpose(0, 1, 3, 2))
    if fmt == "e4m3":
        words = by_word.astype(ml_dtypes.float8_e4m3fn).view(np.uint8)
    else:
        c = by_word.astype(ml_dtypes.float4_e2m1fn).view(np.uint8) & 0xF
        words = (c[..., 0::2] | (c[..., 1::2] << 4)).reshape(k // 512, 128, 2 * n)
    return np.ascontiguousarray(words), np.ascontiguousarray(byte.astype(np.uint8).reshape(k // 512, 16, n))


def unpack_weight(words, scales, fmt):
    g, _, n = scales.shape
    words = np.ascontiguousarray(words).reshape(g, 128, n, -1)
    if fmt == "e4m3":
        vals = words.view(ml_dtypes.float8_e4m3fn).astype(np.float64)
    else:
        nib = np.empty((g, 128, n, 4), np.uint8)
        nib[..., 0::2] = words & 0xF
        nib[..., 1::2] = words >> 4
        vals = E2M1[nib]
    vals = vals * np.repeat(np.exp2(scales.astype(np.float64) - 127.0), 8, axis=1)[..., None]
    return vals.transpose(0, 1, 3, 2).reshape(g * 512, n)


def gelu(v):
    return 0.5 * v * (1.0 + np.tanh(np.sqrt(2.0 / np.pi) * (v + 0.044715 * v**3)))


K, K2, H, N, T, TB, S, P = 1024, 512, 1024, 384, 4096, 2048, 1024, 512

def setup_inputs():
    n = np.random.standard_normal
    s, s2, u = mx_kscale(K)[:, None], mx_kscale(K2)[:, None], mx_kscale(H)[:, None]
    d = {}
    d["tab_words"], d["tab_scales"] = pack_weight(n((K, T)) * s, "e4m3")
    d["tab2_words"], d["tab2_scales"] = pack_weight(n((K2, TB)) * s2, "e4m3")
    d["offs"] = striped(np.random.permutation(T)[:S])
    d["offs2"] = striped(np.random.permutation(TB)[:P])
    d["pos1"] = striped(np.random.permutation(S)[:P])
    d["wa"] = (0.32 * n((K, H)) / K ** 0.5 / s).astype(np.float32)
    d["phase"] = np.random.uniform(-1.2, 1.2, H).astype(np.float32)
    d["gain"] = (np.exp(0.3 * n(H)) * u[:, 0]).astype(np.float32)
    d["wb_words"], d["wb_scales"] = pack_weight(0.9 * n((K2, H)) / K2 ** 0.5 / s2 * u.T, "e2m1")
    d["wgs"] = np.exp(0.3 * n((128, P))).astype(np.float32)
    d["w1"] = (1.5 * n((H, N)) / H ** 0.5 / u).astype(np.float32)
    d["w2_words"], d["w2_scales"] = pack_weight(1.3 * n((H, N)) / H ** 0.5 / u, "e2m1")
    return d

def reference(tab_words, tab_scales, tab2_words, tab2_scales, offs, offs2, pos1, wa, phase, gain,
              wb_words, wb_scales, wgs, w1, w2_words, w2_scales):
    v = unpack_weight(tab_words, tab_scales, "e4m3")[:, unstriped(offs)]
    v2 = unpack_weight(tab2_words, tab2_scales, "e4m3")[:, unstriped(offs2)]
    wb = unpack_weight(wb_words, wb_scales, "e2m1")
    w2 = unpack_weight(w2_words, w2_scales, "e2m1")
    ya = mxq(f64(wa), 0, "e4m3").T @ v
    a = f64(gain)[:, None] * np.cos(ya + f64(phase)[:, None])
    b = wb.T @ v2
    placed = np.zeros((H, S))
    placed[:, unstriped(pos1)] = np.tile(f64(wgs), (H // 128, 1)) * b
    z = a - placed
    zq = mxq(z, 0, "e4m3")
    tone = mxq(f64(w1), 0, "e4m3").T @ zq
    drift = w2.T @ zq
    return tone / (1.0 + np.abs(drift))

@@ -1,0 +1,334 @@
+import math
+from contextlib import ExitStack
+
+import concourse.mybir as mybir
+
+K, K2, H, N, T, TB, S, PL = 1024, 512, 1024, 384, 4096, 2048, 1024, 512
+FLOPS = 2 * (K * H * S + K2 * H * PL + 2 * H * N * S)
+
+F32 = mybir.dt.float32
+BF16 = mybir.dt.bfloat16
+I32 = mybir.dt.int32
+U32 = mybir.dt.uint32
+U16 = mybir.dt.uint16
+U8 = mybir.dt.uint8
+FP8X4 = mybir.dt.float8_e4m3fn_x4
+FP4X4 = mybir.dt.float4_e2m1fn_x4
+ALU = mybir.AluOpType
+ACT = mybir.ActivationFunctionType
+
+P = 128
+W = 512
+TURN = 2.0 * math.pi
+ROUNDER = 12582912.0
+
+AMODE = "SVSVSSVV"
+WA_AT = [0, 1]
+W1_AT = [4, 5]
+PB = 3
+ILENG = "SSVV"
+SQ = "VVVVVV"
+
+
+def tile_list_reed_tone_scorer_kernel(
+    tc, tab_words, tab_scales, tab2_words, tab2_scales, offs, offs2, pos1, wa, phase, gain,
+    wb_words, wb_scales, wgs, w1, w2_words, w2_scales, out,
+):
+    nc = tc.nc
+    with ExitStack() as ctx:
+        keep = ctx.enter_context(tc.tile_pool(name="keep", bufs=1))
+        psum = ctx.enter_context(tc.psum_pool(name="psum", bufs=1))
+
+        def sb(name, shape, dtype):
+            return keep.tile(shape, dtype, name=name, align_bytes=64)
+
+        def ring(name, count, shape, dtype):
+            return [sb(name + str(i), shape, dtype) for i in range(count)]
+
+        banks = [psum.tile([P, W], F32, name="bank" + str(i)) for i in range(8)]
+
+        offs_t = sb("offs_t", [P, S // 16], U16)
+        offs2_t = sb("offs2_t", [P, PL // 16], U16)
+        pos_t = sb("pos_t", [P, PL // 16], U16)
+        tabw = ring("tabw", 2, [P, T], I32)
+        tabs = sb("tabs", [P, T], U8)
+        tab2w = sb("tab2w", [P, TB], I32)
+        tab2s = sb("tab2s", [P, TB], U8)
+        wbw = sb("wbw", [P, 2 * H], U8)
+        wbs = sb("wbs", [P, H], U8)
+        wbw_d = ring("wbw_d", 2, [P, H], U8)
+        wbs_d = ring("wbs_d", 2, [P, W], U8)
+        wgs_t = sb("wgs_t", [P, 4 * PL], F32)
+        raw = ring("raw", 4, [P, 4 * W], F32)
+        woven = ring("woven", 3, [P, 4 * W], BF16)
+        wa_c = ring("wa_c", 4, [P, W], U32)
+        wa_s = ring("wa_s", 4, [P, W], U8)
+        w1_c = ring("w1_c", 2, [P, N], U32)
+        w1_s = ring("w1_s", 2, [P, N], U8)
+        w2w = sb("w2w", [P, 2, 2 * N], U8)
+        w2s = sb("w2s", [P, 2, N], U8)
+        ph = sb("ph", [P, 2, 4], F32)
+        gn = sb("gn", [P, 2, 4], F32)
+        ph_turn = sb("ph_turn", [P, 8], F32)
+        ph_rad = sb("ph_rad", [P, 8], F32)
+        one = sb("one", [P, 1], F32)
+        warm = sb("warm", [P, 1], F32)
+        vw = ring("vw", 4, [P, W], U32)
+        vs = ring("vs", 2, [P, W], U8)
+        v2w = sb("v2w", [P, PL], U32)
+        v2s = sb("v2s", [P, PL], U8)
+        pages = ring("page", 8, [P, S], F32)
+        bsb = ring("bsb", 2, [P, PL], F32)
+        tt = ring("tt", 3, [P, 2 * W], F32)
+        nn = ring("nn", 2, [P, 2 * W], I32)
+        ss = ring("ss", 2, [P, 2 * W], F32)
+        zt = ring("zt", 2, [P, 4 * W], BF16)
+        z_c = ring("z_c", 4, [P, W], U32)
+        z_s = ring("z_s", 4, [P, W], U8)
+        qq = ring("qq", 3, [P, W], F32)
+        oo = ring("oo", 3, [P, W], F32)
+
+        def words(ap):
+            return ap.rearrange("p t i -> p (t i)").bitcast(I32)
+
+        nc.gpsimd.memset(tabs[:].bitcast(I32), 0)
+        nc.gpsimd.memset(w2s[:].bitcast(I32), 0)
+        nc.vector.memset(one[:], 1.0)
+        nc.scalar.activation(warm[:], one[:], ACT.Sin)
+        for page in pages:
+            nc.vector.memset(page[:], 0.0)
+
+        def load_plane(tile, rows, q):
+            nc.sync.dma_start(
+                tile[32 * q : 32 * q + 32, :].bitcast(I32),
+                rows[0, 4 * q : 4 * q + 4, :].bitcast(I32).partition_broadcast(8),
+            )
+
+        def load_wa(b, a):
+            nc.sync.dma_start(
+                raw[2 * b + a][:].rearrange("p (j c) -> p j c", j=4),
+                wa[512 * a : 512 * a + 512, 512 * b : 512 * b + 512].rearrange("(p j) c -> p j c", j=4),
+            )
+
+        nc.sync.dma_start(offs2_t[:], offs2)
+        for q in range(4):
+            load_plane(tab2s, tab2_scales, q)
+        load_plane(wbs, wb_scales, 0)
+        nc.sync.dma_start(wbw[:].bitcast(I32), wb_words[0].bitcast(I32))
+        nc.sync.dma_start(tab2w[:], words(tab2_words[0]))
+        for q in range(1, 4):
+            load_plane(wbs, wb_scales, q)
+        nc.sync.dma_start(pos_t[:], pos1)
+        for q in range(4):
+            nc.sync.dma_start(wgs_t[32 * q : 32 * q + 32, :], wgs.rearrange("(m t) j -> m (t j)", t=4))
+        load_wa(0, 0)
+        load_wa(0, 1)
+        nc.sync.dma_start(offs_t[:], offs)
+        for q in range(4):
+            nc.sync.dma_start(
+                tabs[32 * q : 32 * q + 8, :].bitcast(I32), tab_scales[:, 4 * q : 4 * q + 4, :].bitcast(I32)
+            )
+        nc.sync.dma_start(ph[:], phase.rearrange("(b p t) -> p b t", b=2, t=4))
+        for a in range(2):
+            nc.sync.dma_start(tabw[a][:], words(tab_words[a]))
+        nc.sync.dma_start(gn[:], gain.rearrange("(b p t) -> p b t", b=2, t=4))
+        load_wa(1, 0)
+        load_wa(1, 1)
+        nc.sync.dma_start(w2w[:].bitcast(I32), w2_words.rearrange("a p c -> p a c").bitcast(I32))
+        for q in range(4):
+            nc.sync.dma_start(
+                w2s[32 * q : 32 * q + 4, :, :].bitcast(I32),
+                w2_scales[:, 4 * q : 4 * q + 4, :].rearrange("a r n -> r a n").bitcast(I32),
+            )
+
+        nc.vector.tensor_copy(v2s[:], tab2s[:].indirect(offs2_t[:]))
+        nc.vector.tensor_copy(v2w[:], tab2w[:].bitcast(U32).indirect(offs2_t[:]))
+
+        def deal_wb(b):
+            nc.vector.tensor_copy(
+                wbw_d[b][:].rearrange("p (t m e) -> p m t e", t=4, e=2),
+                wbw[:, H * b : H * b + H].rearrange("p (m t e) -> p m t e", t=4, e=2),
+            )
+            nc.vector.tensor_copy(
+                wbs_d[b][:].rearrange("p (t m) -> p m t", t=4),
+                wbs[:, W * b : W * b + W].rearrange("p (m t) -> p m t", t=4),
+            )
+
+        def place(i, bank):
+            b, t = divmod(i, 4)
+            nc.tensor.matmul_mx(
+                bank[:],
+                lhsT=wbw_d[b][:, 256 * t : 256 * t + 256].bitcast(FP4X4),
+                lhsT_scale=wbs_d[b][:, P * t : P * t + P],
+                rhs=v2w[:].bitcast(FP8X4),
+                rhs_scale=v2s[:],
+                start=True,
+                stop=True,
+            )
+            held = bsb[i % 2]
+            nc.scalar.copy(held[:], bank[:])
+            nc.vector.tensor_tensor(
+                pages[i][:].indirect(pos_t[:]), held[:], wgs_t[:, PL * t : PL * t + PL], ALU.mult
+            )
+
+        def quantize_wa(b, a, slot):
+            i = 2 * b + a
+            nc.scalar.copy(
+                woven[slot][:].rearrange("p (t m j) -> p m j t", t=4, j=4),
+                raw[i][:].rearrange("p (j m t) -> p m j t", j=4, t=4),
+            )
+            nc.vector.quantize_mx(wa_c[i][:].bitcast(FP8X4), wa_s[i][:], woven[slot][:])
+
+        def quantize_w1(a, slot):
+            nc.sync.dma_start(
+                raw[a][:, 0 : 4 * N], w1[512 * a : 512 * a + 512, :].rearrange("(p j) n -> p (j n)", j=4)
+            )
+            nc.scalar.copy(
+                woven[slot][:, 0 : 4 * N].rearrange("p (c i j) -> p c j i", i=4, j=4),
+                raw[a][:, 0 : 4 * N].rearrange("p (j c i) -> p c j i", j=4, i=4),
+            )
+            nc.vector.quantize_mx(w1_c[a][:, 0:256].bitcast(FP8X4), w1_s[a][:, 0:256], woven[slot][:, 0:1024])
+            nc.vector.quantize_mx(w1_c[a][:, 256:N].bitcast(FP8X4), w1_s[a][:, 256:N], woven[slot][:, 1024 : 4 * N])
+
+        def gather_tab(h):
+            cut = offs_t[:, 32 * h : 32 * h + 32]
+            nc.vector.tensor_copy(vw[2 * h][:], tabw[0][:].bitcast(U32).indirect(cut))
+            nc.vector.tensor_copy(vs[h][:], tabs[:].indirect(cut))
+            nc.vector.tensor_copy(vw[2 * h + 1][:], tabw[1][:].bitcast(U32).indirect(cut))
+
+        def phase_mm(b, h, t, bank):
+            for a in range(2):
+                nc.tensor.matmul_mx(
+                    bank[:],
+                    lhsT=wa_c[2 * b + a][:, P * t : P * t + P].bitcast(FP8X4),
+                    lhsT_scale=wa_s[2 * b + a][:, P * t : P * t + P],
+                    rhs=vw[2 * h + a][:].bitcast(FP8X4),
+                    rhs_scale=vs[h][4 * a : P, :],
+                    start=(a == 0),
+                    stop=(a == 1),
+                )
+
+        def reduce_angle(step):
+            u, pair = divmod(step, 2)
+            b, h = divmod(u, 2)
+            mode = AMODE[step]
+            turns, whole = tt[step % 3], nn[step % 2]
+            for e in range(2):
+                t = 2 * pair + e
+                bank = banks[(2 * step + e) % 4]
+                cols = slice(W * e, W * e + W)
+                i = 4 * b + t
+                phase_mm(b, h, t, bank)
+                if mode == "V":
+                    nc.vector.tensor_scalar(
+                        whole[:, cols], bank[:], 1.0 / TURN, ph_turn[:, i : i + 1], ALU.mult, ALU.add
+                    )
+                    nc.vector.scalar_tensor_tensor(
+                        turns[:, cols], bank[:], 1.0 / TURN, whole[:, cols], ALU.mult, ALU.subtract
+                    )
+                else:
+                    nc.scalar.activation(
+                        turns[:, cols], bank[:], ACT.Identity, bias=ph_turn[:, i : i + 1], scale=1.0 / TURN
+                    )
+            if mode == "S":
+                nc.scalar.activation(whole[:].bitcast(U32), turns[:], ACT.Copy, bias=ROUNDER, scale=1.0)
+                nc.vector.scalar_tensor_tensor(turns[:], whole[:], ROUNDER, turns[:], ALU.subtract, ALU.subtract)
+            if mode == "M":
+                nc.vector.tensor_scalar(whole[:], turns[:], ROUNDER, ROUNDER, ALU.add, ALU.subtract)
+                nc.vector.tensor_tensor(turns[:], whole[:], turns[:], ALU.subtract)
+
+        def features(step):
+            u, pair = divmod(step, 2)
+            b, h = divmod(u, 2)
+            turns, sines = tt[step % 3], ss[step % 2]
+            if AMODE[step] != "V":
+                nc.scalar.activation(sines[:], turns[:], ACT.Sin, scale=-TURN)
+            for e in range(2):
+                t = 2 * pair + e
+                i = 4 * b + t
+                cols = slice(W * e, W * e + W)
+                if AMODE[step] == "V":
+                    nc.scalar.activation(
+                        sines[:, cols], turns[:, cols], ACT.Sin, bias=ph_rad[:, i : i + 1], scale=TURN
+                    )
+                nc.vector.scalar_tensor_tensor(
+                    zt[u % 2][:, W * t : W * t + W],
+                    sines[:, cols],
+                    gn[:, b, t : t + 1],
+                    pages[i][:, W * h : W * h + W],
+                    ALU.mult,
+                    ALU.subtract,
+                )
+
+        def quantize_z(u, slot):
+            dst = woven[slot][:].rearrange("p (c i t) -> p c t i", i=4, t=4)
+            src = zt[u % 2][:].rearrange("p (t c i) -> p c t i", t=4, i=4)
+            if ILENG[u] == "S":
+                nc.scalar.copy(dst, src)
+            else:
+                nc.vector.tensor_copy(dst, src)
+            nc.vector.quantize_mx(z_c[u][:].bitcast(FP8X4), z_s[u][:], woven[slot][:])
+
+        def score(h, m, tone, drift):
+            cols = slice(P * m, P * m + P)
+            for b in range(2):
+                nc.tensor.matmul_mx(
+                    drift[:],
+                    lhsT=w2w[:, b, 256 * m : 256 * m + 256].bitcast(FP4X4),
+                    lhsT_scale=w2s[:, b, cols],
+                    rhs=z_c[2 * b + h][:].bitcast(FP8X4),
+                    rhs_scale=z_s[2 * b + h][:],
+                    start=(b == 0),
+                    stop=(b == 1),
+                )
+            for b in range(2):
+                nc.tensor.matmul_mx(
+                    tone[:],
+                    lhsT=w1_c[b][:, cols].bitcast(FP8X4),
+                    lhsT_scale=w1_s[b][:, cols],
+                    rhs=z_c[2 * b + h][:].bitcast(FP8X4),
+                    rhs_scale=z_s[2 * b + h][:],
+                    start=(b == 0),
+                    stop=(b == 1),
+                )
+            i = 3 * h + m
+            size, root, res = qq[i % 3][:], tt[7 % 3][:, W * (i % 2) : W * (i % 2) + W], oo[i % 3]
+            nc.scalar.activation(size, drift[:], ACT.Abs)
+            nc.scalar.activation(root, size, ACT.Abs_reciprocal_sqrt, bias=one[:])
+            if SQ[i] == "S":
+                nc.scalar.activation(root, root, ACT.Square)
+                nc.vector.tensor_tensor(res[:], tone[:], root, ALU.mult)
+            else:
+                nc.vector.tensor_tensor(res[:], tone[:], root, ALU.mult)
+                nc.vector.tensor_tensor(res[:], res[:], root, ALU.mult)
+            nc.sync.dma_start(out[cols, W * h : W * h + W], res[:])
+
+        deal_wb(0)
+        for i in range(2):
+            place(i, banks[4 + i])
+        deal_wb(1)
+        quantize_wa(0, 0, 0)
+        quantize_wa(0, 1, 1)
+        flat_phase = ph[:].rearrange("p b t -> p (b t)")
+        nc.vector.tensor_scalar(ph_turn[:], flat_phase, 1.0 / TURN, 0.25, ALU.mult, ALU.add)
+        nc.vector.tensor_scalar(ph_rad[:], flat_phase, 1.0, math.pi / 2, ALU.mult, ALU.add)
+        gather_tab(0)
+        gather_tab(1)
+
+        reduce_angle(0)
+        for step in range(8):
+            if step < 7:
+                reduce_angle(step + 1)
+            if step < 6:
+                place(step + 2, banks[(2 * step + PB) % 4])
+            features(step)
+            if step % 2 == 1:
+                quantize_z(step // 2, 1)
+            if step in WA_AT:
+                quantize_wa(1, WA_AT.index(step), 2 * (1 - WA_AT.index(step)))
+            if step in W1_AT:
+                quantize_w1(W1_AT.index(step), 2 * W1_AT.index(step))
+        for h in range(2):
+            for m in range(3):
+                i = 3 * h + m
+                score(h, m, banks[(2 * i + 4) % 8], banks[(2 * i + 5) % 8])

@@ -22,12 +22,13 @@ W = 512
 TURN = 2.0 * math.pi
 ROUNDER = 12582912.0
 
-AMODE = "SVSVSSVV"
-WA_AT = [0, 1]
-W1_AT = [4, 5]
-PB = 3
-ILENG = "SSVV"
-SQ = "VVVVVV"
+STEPS = 8
+PAGES = 6
+VECTOR_PAGES = 4
+EARLY_SLICES = 3
+WGS_AHEAD = 2
+W1_STEP = 4
+VECTOR_SQUARES = 4
 
 
 def tile_list_reed_tone_scorer_kernel(
@@ -42,7 +43,7 @@ def tile_list_reed_tone_scorer_kernel(
         def sb(name, shape, dtype):
             return keep.tile(shape, dtype, name=name, align_bytes=64)
 
-        def ring(name, count, shape, dtype):
+        def several(name, count, shape, dtype):
             return [sb(name + str(i), shape, dtype) for i in range(count)]
 
         banks = [psum.tile([P, W], F32, name="bank" + str(i)) for i in range(8)]
@@ -50,88 +51,95 @@ def tile_list_reed_tone_scorer_kernel(
         offs_t = sb("offs_t", [P, S // 16], U16)
         offs2_t = sb("offs2_t", [P, PL // 16], U16)
         pos_t = sb("pos_t", [P, PL // 16], U16)
-        tabw = ring("tabw", 2, [P, T], I32)
+        tabw = several("tabw", 2, [P, T], I32)
         tabs = sb("tabs", [P, T], U8)
         tab2w = sb("tab2w", [P, TB], I32)
         tab2s = sb("tab2s", [P, TB], U8)
         wbw = sb("wbw", [P, 2 * H], U8)
         wbs = sb("wbs", [P, H], U8)
-        wbw_d = ring("wbw_d", 2, [P, H], U8)
-        wbs_d = ring("wbs_d", 2, [P, W], U8)
-        wgs_t = sb("wgs_t", [P, 4 * PL], F32)
-        raw = ring("raw", 4, [P, 4 * W], F32)
-        woven = ring("woven", 3, [P, 4 * W], BF16)
-        wa_c = ring("wa_c", 4, [P, W], U32)
-        wa_s = ring("wa_s", 4, [P, W], U8)
-        w1_c = ring("w1_c", 2, [P, N], U32)
-        w1_s = ring("w1_s", 2, [P, N], U8)
+        wbw_d = several("wbw_d", 2, [P, H], U8)
+        wbs_d = several("wbs_d", 2, [P, W], U8)
+        wgs_t = several("wgs_t", 2, [P, 2 * PL], F32)
+        raw = several("raw", 4, [P, 4 * W], F32)
+        woven = several("woven", 3, [P, 4 * W], BF16)
+        wa_c = several("wa_c", 4, [P, W], U32)
+        wa_s = several("wa_s", 4, [P, W], U8)
+        w1_c = several("w1_c", 2, [P, N], U32)
+        w1_s = several("w1_s", 2, [P, N], U8)
         w2w = sb("w2w", [P, 2, 2 * N], U8)
         w2s = sb("w2s", [P, 2, N], U8)
         ph = sb("ph", [P, 2, 4], F32)
         gn = sb("gn", [P, 2, 4], F32)
         ph_turn = sb("ph_turn", [P, 8], F32)
-        ph_rad = sb("ph_rad", [P, 8], F32)
         one = sb("one", [P, 1], F32)
         warm = sb("warm", [P, 1], F32)
-        vw = ring("vw", 4, [P, W], U32)
-        vs = ring("vs", 2, [P, W], U8)
+        vw = several("vw", 4, [P, W], U32)
+        vs = several("vs", 2, [P, W], U8)
         v2w = sb("v2w", [P, PL], U32)
         v2s = sb("v2s", [P, PL], U8)
-        pages = ring("page", 8, [P, S], F32)
-        bsb = ring("bsb", 2, [P, PL], F32)
-        tt = ring("tt", 3, [P, 2 * W], F32)
-        nn = ring("nn", 2, [P, 2 * W], I32)
-        ss = ring("ss", 2, [P, 2 * W], F32)
-        zt = ring("zt", 2, [P, 4 * W], BF16)
-        z_c = ring("z_c", 4, [P, W], U32)
-        z_s = ring("z_s", 4, [P, W], U8)
-        qq = ring("qq", 3, [P, W], F32)
-        oo = ring("oo", 3, [P, W], F32)
+        pages = several("page", PAGES, [P, S], F32)
+        staged = several("bsb", 4, [P, PL], F32)
+        angles = several("tt", 3, [P, 2 * W], F32)
+        wholes = several("nn", 2, [P, 2 * W], I32)
+        sines = several("ss", 2, [P, 2 * W], F32)
+        zt = several("zt", 2, [P, 4 * W], BF16)
+        z_c = several("z_c", 4, [P, W], U32)
+        z_s = several("z_s", 4, [P, W], U8)
+        sizes = several("qq", 4, [P, W], F32)
+        results = several("oo", 3, [P, W], F32)
+
+        nc.gpsimd.memset(tab2s[:].bitcast(I32), 0)
+        nc.gpsimd.memset(wbs[:].bitcast(I32), 0)
+        nc.gpsimd.memset(tabs[:].bitcast(I32), 0)
+        nc.vector.memset(one[:], 1.0)
+        nc.scalar.activation(warm[:], one[:], ACT.Sin)
+        nc.vector.memset(w2s[:].bitcast(I32), 0)
+        for i, page in enumerate(pages):
+            (nc.vector if i < VECTOR_PAGES else nc.gpsimd).memset(page[:], 0.0)
 
         def words(ap):
             return ap.rearrange("p t i -> p (t i)").bitcast(I32)
 
-        nc.gpsimd.memset(tabs[:].bitcast(I32), 0)
-        nc.gpsimd.memset(w2s[:].bitcast(I32), 0)
-        nc.vector.memset(one[:], 1.0)
-        nc.scalar.activation(warm[:], one[:], ACT.Sin)
-        for page in pages:
-            nc.vector.memset(page[:], 0.0)
+        def load_scale_rows(tile, rows, q, lower=0):
+            first = 32 * q + lower
+            nc.sync.dma_start(tile[first : first + 4, :].bitcast(I32), rows[4 * q : 4 * q + 4, :].bitcast(I32))
 
-        def load_plane(tile, rows, q):
-            nc.sync.dma_start(
-                tile[32 * q : 32 * q + 32, :].bitcast(I32),
-                rows[0, 4 * q : 4 * q + 4, :].bitcast(I32).partition_broadcast(8),
-            )
+        def load_wgs(g, quadrants):
+            rows = wgs.rearrange("(m t) j -> m (t j)", t=4)[:, 2 * PL * g : 2 * PL * g + 2 * PL]
+            for q in quadrants:
+                nc.sync.dma_start(wgs_t[g][32 * q : 32 * q + 32, :], rows)
 
         def load_wa(b, a):
             nc.sync.dma_start(
                 raw[2 * b + a][:].rearrange("p (j c) -> p j c", j=4),
-                wa[512 * a : 512 * a + 512, 512 * b : 512 * b + 512].rearrange("(p j) c -> p j c", j=4),
+                wa[W * a : W * a + W, W * b : W * b + W].rearrange("(p j) c -> p j c", j=4),
             )
 
         nc.sync.dma_start(offs2_t[:], offs2)
         for q in range(4):
-            load_plane(tab2s, tab2_scales, q)
-        load_plane(wbs, wb_scales, 0)
+            load_scale_rows(tab2s, tab2_scales[0], q)
+        load_scale_rows(wbs, wb_scales[0], 0)
         nc.sync.dma_start(wbw[:].bitcast(I32), wb_words[0].bitcast(I32))
         nc.sync.dma_start(tab2w[:], words(tab2_words[0]))
         for q in range(1, 4):
-            load_plane(wbs, wb_scales, q)
+            load_scale_rows(wbs, wb_scales[0], q)
         nc.sync.dma_start(pos_t[:], pos1)
-        for q in range(4):
-            nc.sync.dma_start(wgs_t[32 * q : 32 * q + 32, :], wgs.rearrange("(m t) j -> m (t j)", t=4))
+        load_wgs(0, range(4))
+
         load_wa(0, 0)
-        load_wa(0, 1)
         nc.sync.dma_start(offs_t[:], offs)
         for q in range(4):
-            nc.sync.dma_start(
-                tabs[32 * q : 32 * q + 8, :].bitcast(I32), tab_scales[:, 4 * q : 4 * q + 4, :].bitcast(I32)
-            )
+            load_scale_rows(tabs, tab_scales[0], q)
+        load_wa(0, 1)
+        for q in range(4):
+            load_scale_rows(tabs, tab_scales[1], q, lower=4)
+        nc.sync.dma_start(tabw[0][:], words(tab_words[0]))
         nc.sync.dma_start(ph[:], phase.rearrange("(b p t) -> p b t", b=2, t=4))
-        for a in range(2):
-            nc.sync.dma_start(tabw[a][:], words(tab_words[a]))
         nc.sync.dma_start(gn[:], gain.rearrange("(b p t) -> p b t", b=2, t=4))
+        load_wgs(1, range(WGS_AHEAD))
+        nc.sync.dma_start(tabw[1][:], words(tab_words[1]))
+
+        load_wgs(1, range(WGS_AHEAD, 4))
         load_wa(1, 0)
         load_wa(1, 1)
         nc.sync.dma_start(w2w[:].bitcast(I32), w2_words.rearrange("a p c -> p a c").bitcast(I32))
@@ -141,54 +149,50 @@ def tile_list_reed_tone_scorer_kernel(
                 w2_scales[:, 4 * q : 4 * q + 4, :].rearrange("a r n -> r a n").bitcast(I32),
             )
 
-        nc.vector.tensor_copy(v2s[:], tab2s[:].indirect(offs2_t[:]))
-        nc.vector.tensor_copy(v2w[:], tab2w[:].bitcast(U32).indirect(offs2_t[:]))
-
         def deal_wb(b):
             nc.vector.tensor_copy(
-                wbw_d[b][:].rearrange("p (t m e) -> p m t e", t=4, e=2),
-                wbw[:, H * b : H * b + H].rearrange("p (m t e) -> p m t e", t=4, e=2),
+                wbw_d[b][:].bitcast(U16).rearrange("p (t m) -> p t m", t=4),
+                wbw[:, H * b : H * b + H].bitcast(U16).rearrange("p (m t) -> p t m", t=4),
             )
             nc.vector.tensor_copy(
-                wbs_d[b][:].rearrange("p (t m) -> p m t", t=4),
-                wbs[:, W * b : W * b + W].rearrange("p (m t) -> p m t", t=4),
+                wbs_d[b][:].rearrange("p (t m) -> p t m", t=4),
+                wbs[:, W * b : W * b + W].rearrange("p (m t) -> p t m", t=4),
             )
 
         def place(i, bank):
             b, t = divmod(i, 4)
             nc.tensor.matmul_mx(
                 bank[:],
-                lhsT=wbw_d[b][:, 256 * t : 256 * t + 256].bitcast(FP4X4),
+                lhsT=wbw_d[b][:, 2 * P * t : 2 * P * t + 2 * P].bitcast(FP4X4),
                 lhsT_scale=wbs_d[b][:, P * t : P * t + P],
                 rhs=v2w[:].bitcast(FP8X4),
                 rhs_scale=v2s[:],
                 start=True,
                 stop=True,
             )
-            held = bsb[i % 2]
+            held = staged[i % len(staged)]
             nc.scalar.copy(held[:], bank[:])
-            nc.vector.tensor_tensor(
-                pages[i][:].indirect(pos_t[:]), held[:], wgs_t[:, PL * t : PL * t + PL], ALU.mult
-            )
+            weights = wgs_t[t // 2][:, PL * (t % 2) : PL * (t % 2) + PL]
+            nc.vector.tensor_tensor(pages[i % PAGES][:].indirect(pos_t[:]), held[:], weights, ALU.mult)
 
-        def quantize_wa(b, a, slot):
+        def quantize_wa(b, a, tile):
             i = 2 * b + a
             nc.scalar.copy(
-                woven[slot][:].rearrange("p (t m j) -> p m j t", t=4, j=4),
-                raw[i][:].rearrange("p (j m t) -> p m j t", j=4, t=4),
+                tile[:].rearrange("p (u e m j) -> p u m j e", u=2, e=2, j=4),
+                raw[i][:].rearrange("p (j m u e) -> p u m j e", j=4, u=2, e=2),
             )
-            nc.vector.quantize_mx(wa_c[i][:].bitcast(FP8X4), wa_s[i][:], woven[slot][:])
+            nc.vector.quantize_mx(wa_c[i][:].bitcast(FP8X4), wa_s[i][:], tile[:])
 
-        def quantize_w1(a, slot):
-            nc.sync.dma_start(
-                raw[a][:, 0 : 4 * N], w1[512 * a : 512 * a + 512, :].rearrange("(p j) n -> p (j n)", j=4)
-            )
+        def quantize_w1(a, tile):
+            nc.sync.dma_start(raw[a][:, 0 : 4 * N], w1[W * a : W * a + W, :].rearrange("(p j) n -> p (j n)", j=4))
             nc.scalar.copy(
-                woven[slot][:, 0 : 4 * N].rearrange("p (c i j) -> p c j i", i=4, j=4),
+                tile[:, 0 : 4 * N].rearrange("p (c i j) -> p c j i", i=4, j=4),
                 raw[a][:, 0 : 4 * N].rearrange("p (j c i) -> p c j i", j=4, i=4),
             )
-            nc.vector.quantize_mx(w1_c[a][:, 0:256].bitcast(FP8X4), w1_s[a][:, 0:256], woven[slot][:, 0:1024])
-            nc.vector.quantize_mx(w1_c[a][:, 256:N].bitcast(FP8X4), w1_s[a][:, 256:N], woven[slot][:, 1024 : 4 * N])
+            for first, last in ((0, 256), (256, N)):
+                nc.vector.quantize_mx(
+                    w1_c[a][:, first:last].bitcast(FP8X4), w1_s[a][:, first:last], tile[:, 4 * first : 4 * last]
+                )
 
         def gather_tab(h):
             cut = offs_t[:, 32 * h : 32 * h + 32]
@@ -196,86 +200,61 @@ def tile_list_reed_tone_scorer_kernel(
             nc.vector.tensor_copy(vs[h][:], tabs[:].indirect(cut))
             nc.vector.tensor_copy(vw[2 * h + 1][:], tabw[1][:].bitcast(U32).indirect(cut))
 
-        def phase_mm(b, h, t, bank):
-            for a in range(2):
-                nc.tensor.matmul_mx(
-                    bank[:],
-                    lhsT=wa_c[2 * b + a][:, P * t : P * t + P].bitcast(FP8X4),
-                    lhsT_scale=wa_s[2 * b + a][:, P * t : P * t + P],
-                    rhs=vw[2 * h + a][:].bitcast(FP8X4),
-                    rhs_scale=vs[h][4 * a : P, :],
-                    start=(a == 0),
-                    stop=(a == 1),
-                )
-
         def reduce_angle(step):
-            u, pair = divmod(step, 2)
-            b, h = divmod(u, 2)
-            mode = AMODE[step]
-            turns, whole = tt[step % 3], nn[step % 2]
+            b, h, pair = step // 4, step // 2 % 2, step % 2
+            angle, whole = angles[step % 3], wholes[step % 2]
             for e in range(2):
                 t = 2 * pair + e
-                bank = banks[(2 * step + e) % 4]
-                cols = slice(W * e, W * e + W)
-                i = 4 * b + t
-                phase_mm(b, h, t, bank)
-                if mode == "V":
-                    nc.vector.tensor_scalar(
-                        whole[:, cols], bank[:], 1.0 / TURN, ph_turn[:, i : i + 1], ALU.mult, ALU.add
+                bank = banks[2 * pair + e]
+                for a in range(2):
+                    nc.tensor.matmul_mx(
+                        bank[:],
+                        lhsT=wa_c[2 * b + a][:, P * t : P * t + P].bitcast(FP8X4),
+                        lhsT_scale=wa_s[2 * b + a][:, P * t : P * t + P],
+                        rhs=vw[2 * h + a][:].bitcast(FP8X4),
+                        rhs_scale=vs[h][4 * a : P, :],
+                        start=(a == 0),
+                        stop=(a == 1),
                     )
-                    nc.vector.scalar_tensor_tensor(
-                        turns[:, cols], bank[:], 1.0 / TURN, whole[:, cols], ALU.mult, ALU.subtract
-                    )
-                else:
-                    nc.scalar.activation(
-                        turns[:, cols], bank[:], ACT.Identity, bias=ph_turn[:, i : i + 1], scale=1.0 / TURN
-                    )
-            if mode == "S":
-                nc.scalar.activation(whole[:].bitcast(U32), turns[:], ACT.Copy, bias=ROUNDER, scale=1.0)
-                nc.vector.scalar_tensor_tensor(turns[:], whole[:], ROUNDER, turns[:], ALU.subtract, ALU.subtract)
-            if mode == "M":
-                nc.vector.tensor_scalar(whole[:], turns[:], ROUNDER, ROUNDER, ALU.add, ALU.subtract)
-                nc.vector.tensor_tensor(turns[:], whole[:], turns[:], ALU.subtract)
+                nc.scalar.activation(
+                    angle[:, W * e : W * e + W], bank[:], ACT.Identity,
+                    bias=ph_turn[:, 4 * b + t : 4 * b + t + 1], scale=1.0 / TURN,
+                )
+            nc.scalar.activation(whole[:].bitcast(U32), angle[:], ACT.Copy, bias=ROUNDER, scale=1.0)
+            nc.vector.scalar_tensor_tensor(angle[:], whole[:], ROUNDER, angle[:], ALU.subtract, ALU.subtract)
 
         def features(step):
-            u, pair = divmod(step, 2)
-            b, h = divmod(u, 2)
-            turns, sines = tt[step % 3], ss[step % 2]
-            if AMODE[step] != "V":
-                nc.scalar.activation(sines[:], turns[:], ACT.Sin, scale=-TURN)
+            b, h, pair = step // 4, step // 2 % 2, step % 2
+            sine = sines[step % 2]
+            nc.scalar.activation(sine[:], angles[step % 3][:], ACT.Sin, scale=-TURN)
             for e in range(2):
                 t = 2 * pair + e
-                i = 4 * b + t
-                cols = slice(W * e, W * e + W)
-                if AMODE[step] == "V":
-                    nc.scalar.activation(
-                        sines[:, cols], turns[:, cols], ACT.Sin, bias=ph_rad[:, i : i + 1], scale=TURN
-                    )
                 nc.vector.scalar_tensor_tensor(
-                    zt[u % 2][:, W * t : W * t + W],
-                    sines[:, cols],
+                    zt[h][:, W * t : W * t + W],
+                    sine[:, W * e : W * e + W],
                     gn[:, b, t : t + 1],
-                    pages[i][:, W * h : W * h + W],
+                    pages[(4 * b + t) % PAGES][:, W * h : W * h + W],
                     ALU.mult,
                     ALU.subtract,
                 )
 
-        def quantize_z(u, slot):
-            dst = woven[slot][:].rearrange("p (c i t) -> p c t i", i=4, t=4)
-            src = zt[u % 2][:].rearrange("p (t c i) -> p c t i", t=4, i=4)
-            if ILENG[u] == "S":
-                nc.scalar.copy(dst, src)
-            else:
-                nc.vector.tensor_copy(dst, src)
-            nc.vector.quantize_mx(z_c[u][:].bitcast(FP8X4), z_s[u][:], woven[slot][:])
+        def quantize_z(b, h):
+            weave = nc.scalar.copy if b == 0 else nc.vector.tensor_copy
+            weave(
+                woven[1][:].rearrange("p (c i t) -> p c t i", i=4, t=4),
+                zt[h][:].rearrange("p (t c i) -> p c t i", t=4, i=4),
+            )
+            nc.vector.quantize_mx(z_c[2 * b + h][:].bitcast(FP8X4), z_s[2 * b + h][:], woven[1][:])
 
-        def score(h, m, tone, drift):
-            cols = slice(P * m, P * m + P)
+        def score(h, m):
+            i = 3 * h + m
+            rows = slice(P * m, P * m + P)
+            tone, drift = banks[4 - 4 * h + m], banks[7 - 4 * (i % 2)]
             for b in range(2):
                 nc.tensor.matmul_mx(
                     drift[:],
-                    lhsT=w2w[:, b, 256 * m : 256 * m + 256].bitcast(FP4X4),
-                    lhsT_scale=w2s[:, b, cols],
+                    lhsT=w2w[:, b, 2 * P * m : 2 * P * m + 2 * P].bitcast(FP4X4),
+                    lhsT_scale=w2s[:, b, rows],
                     rhs=z_c[2 * b + h][:].bitcast(FP8X4),
                     rhs_scale=z_s[2 * b + h][:],
                     start=(b == 0),
@@ -284,51 +263,53 @@ def tile_list_reed_tone_scorer_kernel(
             for b in range(2):
                 nc.tensor.matmul_mx(
                     tone[:],
-                    lhsT=w1_c[b][:, cols].bitcast(FP8X4),
-                    lhsT_scale=w1_s[b][:, cols],
+                    lhsT=w1_c[b][:, rows].bitcast(FP8X4),
+                    lhsT_scale=w1_s[b][:, rows],
                     rhs=z_c[2 * b + h][:].bitcast(FP8X4),
                     rhs_scale=z_s[2 * b + h][:],
                     start=(b == 0),
                     stop=(b == 1),
                 )
-            i = 3 * h + m
-            size, root, res = qq[i % 3][:], tt[7 % 3][:, W * (i % 2) : W * (i % 2) + W], oo[i % 3]
-            nc.scalar.activation(size, drift[:], ACT.Abs)
-            nc.scalar.activation(root, size, ACT.Abs_reciprocal_sqrt, bias=one[:])
-            if SQ[i] == "S":
-                nc.scalar.activation(root, root, ACT.Square)
-                nc.vector.tensor_tensor(res[:], tone[:], root, ALU.mult)
+            spent = (angles[(STEPS - 1) % 3], sines[(STEPS - 1) % 2])[i // 2 % 2]
+            size, root, result = sizes[i % 4], spent[:, W * (i % 2) : W * (i % 2) + W], results[i % 3]
+            nc.scalar.activation(size[:], drift[:], ACT.Abs)
+            nc.scalar.activation(root, size[:], ACT.Abs_reciprocal_sqrt, bias=one[:])
+            if i < VECTOR_SQUARES:
+                nc.vector.tensor_tensor(result[:], tone[:], root, ALU.mult)
+                nc.vector.tensor_tensor(result[:], result[:], root, ALU.mult)
             else:
-                nc.vector.tensor_tensor(res[:], tone[:], root, ALU.mult)
-                nc.vector.tensor_tensor(res[:], res[:], root, ALU.mult)
-            nc.sync.dma_start(out[cols, W * h : W * h + W], res[:])
+                nc.scalar.activation(root, root, ACT.Square)
+                nc.vector.tensor_tensor(result[:], tone[:], root, ALU.mult)
+            nc.sync.dma_start(out[rows, W * h : W * h + W], result[:])
 
+        nc.vector.tensor_copy(v2s[:], tab2s[:].indirect(offs2_t[:]))
+        nc.vector.tensor_copy(v2w[:], tab2w[:].bitcast(U32).indirect(offs2_t[:]))
         deal_wb(0)
-        for i in range(2):
-            place(i, banks[4 + i])
         deal_wb(1)
-        quantize_wa(0, 0, 0)
-        quantize_wa(0, 1, 1)
-        flat_phase = ph[:].rearrange("p b t -> p (b t)")
-        nc.vector.tensor_scalar(ph_turn[:], flat_phase, 1.0 / TURN, 0.25, ALU.mult, ALU.add)
-        nc.vector.tensor_scalar(ph_rad[:], flat_phase, 1.0, math.pi / 2, ALU.mult, ALU.add)
+        for i in range(EARLY_SLICES):
+            place(i, banks[4 + i])
+        quantize_wa(0, 0, woven[0])
+        quantize_wa(0, 1, woven[1])
+        nc.vector.tensor_scalar(
+            ph_turn[:], ph[:].rearrange("p b t -> p (b t)"), 1.0 / TURN, 0.25, ALU.mult, ALU.add
+        )
         gather_tab(0)
         gather_tab(1)
 
         reduce_angle(0)
-        for step in range(8):
-            if step < 7:
+        for step in range(STEPS):
+            if step + 1 < STEPS:
                 reduce_angle(step + 1)
-            if step < 6:
-                place(step + 2, banks[(2 * step + PB) % 4])
+            if EARLY_SLICES + step < 8:
+                place(EARLY_SLICES + step, banks[2 * ((step + 1) % 2)])
             features(step)
-            if step % 2 == 1:
-                quantize_z(step // 2, 1)
-            if step in WA_AT:
-                quantize_wa(1, WA_AT.index(step), 2 * (1 - WA_AT.index(step)))
-            if step in W1_AT:
-                quantize_w1(W1_AT.index(step), 2 * W1_AT.index(step))
+            if step % 2 == 0 and step > 0:
+                quantize_z(*divmod(step // 2 - 1, 2))
+            if step < 2:
+                quantize_wa(1, step, woven[2 - 2 * step])
+            if W1_STEP <= step < W1_STEP + 2:
+                quantize_w1(step - W1_STEP, woven[2 * (step - W1_STEP)])
+        quantize_z(1, 1)
         for h in range(2):
             for m in range(3):
-                i = 3 * h + m
-                score(h, m, banks[(2 * i + 4) % 8], banks[(2 * i + 5) % 8])
+                score(h, m)

@@ -24,10 +24,9 @@ ROUNDER = 12582912.0
 
 STEPS = 8
 PAGES = 6
-VECTOR_PAGES = 4
 EARLY_SLICES = 3
 WGS_AHEAD = 2
-W1_STEP = 4
+W1_STEP = 5
 VECTOR_SQUARES = 4
 
 
@@ -72,7 +71,7 @@ def tile_list_reed_tone_scorer_kernel(
         gn = sb("gn", [P, 2, 4], F32)
         ph_turn = sb("ph_turn", [P, 8], F32)
         one = sb("one", [P, 1], F32)
-        warm = sb("warm", [P, 1], F32)
+        quarters = sb("quarters", [P, 1], F32)
         vw = several("vw", 4, [P, W], U32)
         vs = several("vs", 2, [P, W], U8)
         v2w = sb("v2w", [P, PL], U32)
@@ -90,12 +89,12 @@ def tile_list_reed_tone_scorer_kernel(
 
         nc.gpsimd.memset(tab2s[:].bitcast(I32), 0)
         nc.gpsimd.memset(wbs[:].bitcast(I32), 0)
-        nc.gpsimd.memset(tabs[:].bitcast(I32), 0)
-        nc.vector.memset(one[:], 1.0)
-        nc.scalar.activation(warm[:], one[:], ACT.Sin)
+        nc.vector.memset(quarters[:], 1.0)
+        nc.scalar.activation(one[:], quarters[:], ACT.Sin, scale=TURN / 4)
+        nc.vector.memset(tabs[:].bitcast(I32), 0)
         nc.vector.memset(w2s[:].bitcast(I32), 0)
-        for i, page in enumerate(pages):
-            (nc.vector if i < VECTOR_PAGES else nc.gpsimd).memset(page[:], 0.0)
+        for page in pages:
+            nc.vector.memset(page[:], 0.0)
 
         def words(ap):
             return ap.rearrange("p t i -> p (t i)").bitcast(I32)

import math
from contextlib import ExitStack

import concourse.mybir as mybir

K, K2, H, N, T, TB, S, PL = 1024, 512, 1024, 384, 4096, 2048, 1024, 512
FLOPS = 2 * (K * H * S + K2 * H * PL + 2 * H * N * S)

F32 = mybir.dt.float32
BF16 = mybir.dt.bfloat16
I32 = mybir.dt.int32
U32 = mybir.dt.uint32
U16 = mybir.dt.uint16
U8 = mybir.dt.uint8
FP8X4 = mybir.dt.float8_e4m3fn_x4
FP4X4 = mybir.dt.float4_e2m1fn_x4
ALU = mybir.AluOpType
ACT = mybir.ActivationFunctionType

P = 128
W = 512
TURN = 2.0 * math.pi
ROUNDER = 12582912.0

STEPS = 8
PAGES = 6
EARLY_SLICES = 3
WGS_AHEAD = 2
W1_STEP = 5
VECTOR_SQUARES = 4


def tile_list_reed_tone_scorer_kernel(
    tc, tab_words, tab_scales, tab2_words, tab2_scales, offs, offs2, pos1, wa, phase, gain,
    wb_words, wb_scales, wgs, w1, w2_words, w2_scales, out,
):
    nc = tc.nc
    with ExitStack() as ctx:
        keep = ctx.enter_context(tc.tile_pool(name="keep", bufs=1))
        psum = ctx.enter_context(tc.psum_pool(name="psum", bufs=1))

        def sb(name, shape, dtype):
            return keep.tile(shape, dtype, name=name, align_bytes=64)

        def several(name, count, shape, dtype):
            return [sb(name + str(i), shape, dtype) for i in range(count)]

        banks = [psum.tile([P, W], F32, name="bank" + str(i)) for i in range(8)]

        offs_t = sb("offs_t", [P, S // 16], U16)
        offs2_t = sb("offs2_t", [P, PL // 16], U16)
        pos_t = sb("pos_t", [P, PL // 16], U16)
        tabw = several("tabw", 2, [P, T], I32)
        tabs = sb("tabs", [P, T], U8)
        tab2w = sb("tab2w", [P, TB], I32)
        tab2s = sb("tab2s", [P, TB], U8)
        wbw = sb("wbw", [P, 2 * H], U8)
        wbs = sb("wbs", [P, H], U8)
        wbw_d = several("wbw_d", 2, [P, H], U8)
        wbs_d = several("wbs_d", 2, [P, W], U8)
        wgs_t = several("wgs_t", 2, [P, 2 * PL], F32)
        raw = several("raw", 4, [P, 4 * W], F32)
        woven = several("woven", 3, [P, 4 * W], BF16)
        wa_c = several("wa_c", 4, [P, W], U32)
        wa_s = several("wa_s", 4, [P, W], U8)
        w1_c = several("w1_c", 2, [P, N], U32)
        w1_s = several("w1_s", 2, [P, N], U8)
        w2w = sb("w2w", [P, 2, 2 * N], U8)
        w2s = sb("w2s", [P, 2, N], U8)
        ph = sb("ph", [P, 2, 4], F32)
        gn = sb("gn", [P, 2, 4], F32)
        ph_turn = sb("ph_turn", [P, 8], F32)
        one = sb("one", [P, 1], F32)
        quarters = sb("quarters", [P, 1], F32)
        vw = several("vw", 4, [P, W], U32)
        vs = several("vs", 2, [P, W], U8)
        v2w = sb("v2w", [P, PL], U32)
        v2s = sb("v2s", [P, PL], U8)
        pages = several("page", PAGES, [P, S], F32)
        staged = several("bsb", 4, [P, PL], F32)
        angles = several("tt", 3, [P, 2 * W], F32)
        wholes = several("nn", 2, [P, 2 * W], I32)
        sines = several("ss", 2, [P, 2 * W], F32)
        zt = several("zt", 2, [P, 4 * W], BF16)
        z_c = several("z_c", 4, [P, W], U32)
        z_s = several("z_s", 4, [P, W], U8)
        sizes = several("qq", 4, [P, W], F32)
        results = several("oo", 3, [P, W], F32)

        nc.gpsimd.memset(tab2s[:].bitcast(I32), 0)
        nc.gpsimd.memset(wbs[:].bitcast(I32), 0)
        nc.vector.memset(quarters[:], 1.0)
        nc.scalar.activation(one[:], quarters[:], ACT.Sin, scale=TURN / 4)
        nc.vector.memset(tabs[:].bitcast(I32), 0)
        nc.vector.memset(w2s[:].bitcast(I32), 0)
        for page in pages:
            nc.vector.memset(page[:], 0.0)

        def words(ap):
            return ap.rearrange("p t i -> p (t i)").bitcast(I32)

        def load_scale_rows(tile, rows, q, lower=0):
            first = 32 * q + lower
            nc.sync.dma_start(tile[first : first + 4, :].bitcast(I32), rows[4 * q : 4 * q + 4, :].bitcast(I32))

        def load_wgs(g, quadrants):
            rows = wgs.rearrange("(m t) j -> m (t j)", t=4)[:, 2 * PL * g : 2 * PL * g + 2 * PL]
            for q in quadrants:
                nc.sync.dma_start(wgs_t[g][32 * q : 32 * q + 32, :], rows)

        def load_wa(b, a):
            nc.sync.dma_start(
                raw[2 * b + a][:].rearrange("p (j c) -> p j c", j=4),
                wa[W * a : W * a + W, W * b : W * b + W].rearrange("(p j) c -> p j c", j=4),
            )

        nc.sync.dma_start(offs2_t[:], offs2)
        for q in range(4):
            load_scale_rows(tab2s, tab2_scales[0], q)
        load_scale_rows(wbs, wb_scales[0], 0)
        nc.sync.dma_start(wbw[:].bitcast(I32), wb_words[0].bitcast(I32))
        nc.sync.dma_start(tab2w[:], words(tab2_words[0]))
        for q in range(1, 4):
            load_scale_rows(wbs, wb_scales[0], q)
        nc.sync.dma_start(pos_t[:], pos1)
        load_wgs(0, range(4))

        load_wa(0, 0)
        nc.sync.dma_start(offs_t[:], offs)
        for q in range(4):
            load_scale_rows(tabs, tab_scales[0], q)
        load_wa(0, 1)
        for q in range(4):
            load_scale_rows(tabs, tab_scales[1], q, lower=4)
        nc.sync.dma_start(tabw[0][:], words(tab_words[0]))
        nc.sync.dma_start(ph[:], phase.rearrange("(b p t) -> p b t", b=2, t=4))
        nc.sync.dma_start(gn[:], gain.rearrange("(b p t) -> p b t", b=2, t=4))
        load_wgs(1, range(WGS_AHEAD))
        nc.sync.dma_start(tabw[1][:], words(tab_words[1]))

        load_wgs(1, range(WGS_AHEAD, 4))
        load_wa(1, 0)
        load_wa(1, 1)
        nc.sync.dma_start(w2w[:].bitcast(I32), w2_words.rearrange("a p c -> p a c").bitcast(I32))
        for q in range(4):
            nc.sync.dma_start(
                w2s[32 * q : 32 * q + 4, :, :].bitcast(I32),
                w2_scales[:, 4 * q : 4 * q + 4, :].rearrange("a r n -> r a n").bitcast(I32),
            )

        def deal_wb(b):
            nc.vector.tensor_copy(
                wbw_d[b][:].bitcast(U16).rearrange("p (t m) -> p t m", t=4),
                wbw[:, H * b : H * b + H].bitcast(U16).rearrange("p (m t) -> p t m", t=4),
            )
            nc.vector.tensor_copy(
                wbs_d[b][:].rearrange("p (t m) -> p t m", t=4),
                wbs[:, W * b : W * b + W].rearrange("p (m t) -> p t m", t=4),
            )

        def place(i, bank):
            b, t = divmod(i, 4)
            nc.tensor.matmul_mx(
                bank[:],
                lhsT=wbw_d[b][:, 2 * P * t : 2 * P * t + 2 * P].bitcast(FP4X4),
                lhsT_scale=wbs_d[b][:, P * t : P * t + P],
                rhs=v2w[:].bitcast(FP8X4),
                rhs_scale=v2s[:],
                start=True,
                stop=True,
            )
            held = staged[i % len(staged)]
            nc.scalar.copy(held[:], bank[:])
            weights = wgs_t[t // 2][:, PL * (t % 2) : PL * (t % 2) + PL]
            nc.vector.tensor_tensor(pages[i % PAGES][:].indirect(pos_t[:]), held[:], weights, ALU.mult)

        def quantize_wa(b, a, tile):
            i = 2 * b + a
            nc.scalar.copy(
                tile[:].rearrange("p (u e m j) -> p u m j e", u=2, e=2, j=4),
                raw[i][:].rearrange("p (j m u e) -> p u m j e", j=4, u=2, e=2),
            )
            nc.vector.quantize_mx(wa_c[i][:].bitcast(FP8X4), wa_s[i][:], tile[:])

        def quantize_w1(a, tile):
            nc.sync.dma_start(raw[a][:, 0 : 4 * N], w1[W * a : W * a + W, :].rearrange("(p j) n -> p (j n)", j=4))
            nc.scalar.copy(
                tile[:, 0 : 4 * N].rearrange("p (c i j) -> p c j i", i=4, j=4),
                raw[a][:, 0 : 4 * N].rearrange("p (j c i) -> p c j i", j=4, i=4),
            )
            for first, last in ((0, 256), (256, N)):
                nc.vector.quantize_mx(
                    w1_c[a][:, first:last].bitcast(FP8X4), w1_s[a][:, first:last], tile[:, 4 * first : 4 * last]
                )

        def gather_tab(h):
            cut = offs_t[:, 32 * h : 32 * h + 32]
            nc.vector.tensor_copy(vw[2 * h][:], tabw[0][:].bitcast(U32).indirect(cut))
            nc.vector.tensor_copy(vs[h][:], tabs[:].indirect(cut))
            nc.vector.tensor_copy(vw[2 * h + 1][:], tabw[1][:].bitcast(U32).indirect(cut))

        def reduce_angle(step):
            b, h, pair = step // 4, step // 2 % 2, step % 2
            angle, whole = angles[step % 3], wholes[step % 2]
            for e in range(2):
                t = 2 * pair + e
                bank = banks[2 * pair + e]
                for a in range(2):
                    nc.tensor.matmul_mx(
                        bank[:],
                        lhsT=wa_c[2 * b + a][:, P * t : P * t + P].bitcast(FP8X4),
                        lhsT_scale=wa_s[2 * b + a][:, P * t : P * t + P],
                        rhs=vw[2 * h + a][:].bitcast(FP8X4),
                        rhs_scale=vs[h][4 * a : P, :],
                        start=(a == 0),
                        stop=(a == 1),
                    )
                nc.scalar.activation(
                    angle[:, W * e : W * e + W], bank[:], ACT.Identity,
                    bias=ph_turn[:, 4 * b + t : 4 * b + t + 1], scale=1.0 / TURN,
                )
            nc.scalar.activation(whole[:].bitcast(U32), angle[:], ACT.Copy, bias=ROUNDER, scale=1.0)
            nc.vector.scalar_tensor_tensor(angle[:], whole[:], ROUNDER, angle[:], ALU.subtract, ALU.subtract)

        def features(step):
            b, h, pair = step // 4, step // 2 % 2, step % 2
            sine = sines[step % 2]
            nc.scalar.activation(sine[:], angles[step % 3][:], ACT.Sin, scale=-TURN)
            for e in range(2):
                t = 2 * pair + e
                nc.vector.scalar_tensor_tensor(
                    zt[h][:, W * t : W * t + W],
                    sine[:, W * e : W * e + W],
                    gn[:, b, t : t + 1],
                    pages[(4 * b + t) % PAGES][:, W * h : W * h + W],
                    ALU.mult,
                    ALU.subtract,
                )

        def quantize_z(b, h):
            weave = nc.scalar.copy if b == 0 else nc.vector.tensor_copy
            weave(
                woven[1][:].rearrange("p (c i t) -> p c t i", i=4, t=4),
                zt[h][:].rearrange("p (t c i) -> p c t i", t=4, i=4),
            )
            nc.vector.quantize_mx(z_c[2 * b + h][:].bitcast(FP8X4), z_s[2 * b + h][:], woven[1][:])

        def score(h, m):
            i = 3 * h + m
            rows = slice(P * m, P * m + P)
            tone, drift = banks[4 - 4 * h + m], banks[7 - 4 * (i % 2)]
            for b in range(2):
                nc.tensor.matmul_mx(
                    drift[:],
                    lhsT=w2w[:, b, 2 * P * m : 2 * P * m + 2 * P].bitcast(FP4X4),
                    lhsT_scale=w2s[:, b, rows],
                    rhs=z_c[2 * b + h][:].bitcast(FP8X4),
                    rhs_scale=z_s[2 * b + h][:],
                    start=(b == 0),
                    stop=(b == 1),
                )
            for b in range(2):
                nc.tensor.matmul_mx(
                    tone[:],
                    lhsT=w1_c[b][:, rows].bitcast(FP8X4),
                    lhsT_scale=w1_s[b][:, rows],
                    rhs=z_c[2 * b + h][:].bitcast(FP8X4),
                    rhs_scale=z_s[2 * b + h][:],
                    start=(b == 0),
                    stop=(b == 1),
                )
            spent = (angles[(STEPS - 1) % 3], sines[(STEPS - 1) % 2])[i // 2 % 2]
            size, root, result = sizes[i % 4], spent[:, W * (i % 2) : W * (i % 2) + W], results[i % 3]
            nc.scalar.activation(size[:], drift[:], ACT.Abs)
            nc.scalar.activation(root, size[:], ACT.Abs_reciprocal_sqrt, bias=one[:])
            if i < VECTOR_SQUARES:
                nc.vector.tensor_tensor(result[:], tone[:], root, ALU.mult)
                nc.vector.tensor_tensor(result[:], result[:], root, ALU.mult)
            else:
                nc.scalar.activation(root, root, ACT.Square)
                nc.vector.tensor_tensor(result[:], tone[:], root, ALU.mult)
            nc.sync.dma_start(out[rows, W * h : W * h + W], result[:])

        nc.vector.tensor_copy(v2s[:], tab2s[:].indirect(offs2_t[:]))
        nc.vector.tensor_copy(v2w[:], tab2w[:].bitcast(U32).indirect(offs2_t[:]))
        deal_wb(0)
        deal_wb(1)
        for i in range(EARLY_SLICES):
            place(i, banks[4 + i])
        quantize_wa(0, 0, woven[0])
        quantize_wa(0, 1, woven[1])
        nc.vector.tensor_scalar(
            ph_turn[:], ph[:].rearrange("p b t -> p (b t)"), 1.0 / TURN, 0.25, ALU.mult, ALU.add
        )
        gather_tab(0)
        gather_tab(1)

        reduce_angle(0)
        for step in range(STEPS):
            if step + 1 < STEPS:
                reduce_angle(step + 1)
            if EARLY_SLICES + step < 8:
                place(EARLY_SLICES + step, banks[2 * ((step + 1) % 2)])
            features(step)
            if step % 2 == 0 and step > 0:
                quantize_z(*divmod(step // 2 - 1, 2))
            if step < 2:
                quantize_wa(1, step, woven[2 - 2 * step])
            if W1_STEP <= step < W1_STEP + 2:
                quantize_w1(step - W1_STEP, woven[2 * (step - W1_STEP)])
        quantize_z(1, 1)
        for h in range(2):
            for m in range(3):
                score(h, m)
